import numpy as np
import ml_dtypes


def mxq(x, axis, fmt="e4m3"):
    dtype, down = {"e4m3": (ml_dtypes.float8_e4m3fn, 7), "e5m2": (ml_dtypes.float8_e5m2, 14)}[fmt]
    v = np.moveaxis(np.asarray(x, np.float32).astype(ml_dtypes.bfloat16).astype(np.float64), axis, -1)
    blocks = v.reshape(v.shape[:-1] + (-1, 32))
    amax = np.abs(blocks).max(-1, keepdims=True)
    byte = np.maximum(np.where(amax > 0, np.frexp(amax)[1] - 1 + 127, 0) - down, 1)
    scale = np.exp2(byte - 127.0)
    codes = (blocks / scale).astype(np.float32).astype(dtype).astype(np.float64)
    return np.moveaxis((codes * scale).reshape(v.shape), -1, axis)


WIDE = False


def mx_kscale(k):
    if not WIDE:
        return np.ones(k)
    levels = np.array([10, -10, 5, -5, 0])
    if k % 512:
        return np.exp2(np.random.permutation(np.resize(levels, k // 32))).repeat(32)
    a = np.empty((k // 512, 16))
    for p in range(k // 512):
        a[p, :8] = np.random.permutation(np.resize(levels, 8))
        for g in range(8):
            far = levels[np.abs(levels - a[p, g]) >= 10]
            a[p, g + 8] = far[np.random.randint(len(far))]
    return np.exp2(a.ravel()).repeat(32)


BF16 = ml_dtypes.bfloat16


def bf(x):
    return np.asarray(x, np.float32).astype(BF16)


def f64(x):
    return np.asarray(x).astype(np.float64)


E2M1 = np.array([0.0, 0.5, 1.0, 1.5, 2.0, 3.0, 4.0, 6.0, -0.0, -0.5, -1.0, -1.5, -2.0, -3.0, -4.0, -6.0])


def pack_weight(w, fmt):
    k, n = w.shape
    w = f64(bf(w)).reshape(k // 32, 32, n)
    amax = np.abs(w).max(1)
    if fmt == "e4m3":
        byte = np.frexp(amax)[1] - 1 + 127 - 7
    else:
        mant, ex = np.frexp(amax / 6.0)
        byte = np.where(mant > 0.5, ex, ex - 1) + 127
    byte = np.clip(np.where(amax > 0, byte, 1), 1, 254)
    scaled = (w * np.exp2(127.0 - byte)[:, None, :]).reshape(k, n).astype(np.float32)
    by_word = np.ascontiguousarray(scaled.reshape(k // 512, 128, 4, n).transpose(0, 1, 3, 2))
    if fmt == "e4m3":
        words = by_word.astype(ml_dtypes.float8_e4m3fn).view(np.uint8)
    else:
        c = by_word.astype(ml_dtypes.float4_e2m1fn).view(np.uint8) & 0xF
        words = c[..., 0::2] | (c[..., 1::2] << 4)
    return np.ascontiguousarray(words), np.ascontiguousarray(byte.astype(np.uint8).reshape(k // 512, 16, n))


def unpack_weight(words, scales, fmt):
    g, p, n, _ = words.shape
    if fmt == "e4m3":
        vals = np.ascontiguousarray(words).view(ml_dtypes.float8_e4m3fn).astype(np.float64)
    else:
        nib = np.empty((g, p, n, 4), np.uint8)
        nib[..., 0::2] = words & 0xF
        nib[..., 1::2] = words >> 4
        vals = E2M1[nib]
    vals = vals * np.repeat(np.exp2(scales.astype(np.float64) - 127.0), 8, axis=1)[..., None]
    return vals.transpose(0, 1, 3, 2).reshape(g * 512, n)
def pack4(w):
    words, scales = pack_weight(w, "e2m1")
    return words.reshape(words.shape[0], 128, -1), scales


def unpack4(words, scales):
    return unpack_weight(words.reshape(words.shape[0], 128, -1, 2), scales, "e2m1")


B, F, C = 1024, 2048, 512


def setup_inputs():
    s = mx_kscale(F)
    u = mx_kscale(B)
    t = mx_kscale(C)
    act = np.tanh(np.random.standard_normal((B, F)))
    v = np.random.standard_normal((F, C)) / np.sqrt(F)
    w = np.random.standard_normal((C, F)) / np.sqrt(C)
    hid_words, hid_scales = pack4(act.T * s[:, None])
    v_words, v_scales = pack4(v / s[:, None])
    w_words, w_scales = pack_weight(w / t[:, None], "e4m3")
    return {"hid_words": hid_words, "hid_scales": hid_scales,
            "v_words": v_words, "v_scales": v_scales,
            "vb": bf(0.3 * np.random.standard_normal(C)),
            "lam": bf(np.random.uniform(0.5, 1.5, (B, C)) * u[:, None] * t),
            "h": bf(act / np.sqrt(B) / u[:, None]),
            "w_words": w_words, "w_scales": w_scales,
            "d": bf((1.0 - act ** 2) / u[:, None])}


def reference(hid_words, hid_scales, v_words, v_scales, vb, lam, h, w_words, w_scales, d):
    z = (unpack4(hid_words, hid_scales).T @ unpack4(v_words, v_scales)) + f64(vb)
    r = f64(lam) * z
    gw = mxq(f64(h), 0, "e4m3").T @ mxq(r, 0, "e4m3")
    ga = f64(d) * (mxq(r, 1, "e4m3") @ unpack_weight(w_words, w_scales, "e4m3"))
    return gw, ga

@@ -1,0 +1,259 @@
+from contextlib import ExitStack
+
+import concourse.mybir as mybir
+from concourse.masks import make_identity
+
+B, F, C = 1024, 2048, 512
+FLOPS = 3 * 2 * B * F * C
+
+F32 = mybir.dt.float32
+BF16 = mybir.dt.bfloat16
+I32 = mybir.dt.int32
+U32 = mybir.dt.uint32
+U8 = mybir.dt.uint8
+FP8X4 = mybir.dt.float8_e4m3fn_x4
+FP4X4 = mybir.dt.float4_e2m1fn_x4
+MULT = mybir.AluOpType.mult
+IDENT = mybir.ActivationFunctionType.Identity
+
+P = 128
+PACK = 4
+KP = P * PACK
+N = 512
+HALVES = B // KP
+FPASS = F // KP
+CT = C // P
+FQ = F // N
+W_ROW0 = 4
+
+
+def tile_gauss_newton_product_s4_kernel(
+    tc, hid_words, hid_scales, v_words, v_scales, vb, lam, h, w_words, w_scales, d, out_0, out_1
+):
+    nc = tc.nc
+    with ExitStack() as ctx:
+        keep = ctx.enter_context(tc.tile_pool(name="keep", bufs=1))
+        work = ctx.enter_context(tc.tile_pool(name="work", bufs=1))
+        psum = ctx.enter_context(tc.psum_pool(name="psum", bufs=1))
+        ctx.enter_context(tc.manual_schedule())
+
+        def kept(name, shape, dtype):
+            return keep.tile(shape, dtype, name=name, align_bytes=64)
+
+        def staged():
+            return work.tile([P, N, PACK], BF16, name="staged", tag="staged", bufs=4, align_bytes=64)
+
+        def scalar_bank():
+            return psum.tile([P, N], F32, name="scalar_bank", tag="scalar_bank", bufs=4)
+
+        def vector_bank():
+            return psum.tile([P, N], F32, name="vector_bank", tag="vector_bank", bufs=4)
+
+        ident = kept("ident", [P, P], F32)
+        vb_rows = kept("vb_rows", [CT, P], BF16)
+        vb_square = kept("vb_square", [P, P], F32)
+        vb_col = kept("vb_col", [P, CT], F32)
+        hid_plane = kept("hid_plane", [P, FPASS, B], U8)
+        v_plane = kept("v_plane", [P, FPASS, C], U8)
+        w_plane = kept("w_plane", [P, F], U8)
+        hid = [kept("hid%d" % g, [P, FPASS, 2 * KP], U8) for g in range(HALVES)]
+        v = kept("v", [P, FPASS, 2 * C], U8)
+        w = kept("w", [P, PACK * F], U8)
+        lam_sb = [kept("lam%d" % g, [P, PACK, C], BF16) for g in range(HALVES)]
+        h_sb = [[kept("h%d_%d" % (g, a), [P, PACK, F // 2], BF16) for a in range(2)] for g in range(HALVES)]
+        d_sb = [[kept("d%d_%d" % (g, a), [P, 2, F], BF16) for a in range(2)] for g in range(HALVES)]
+        zt = [[kept("zt%d_%d" % (g, j), [P, PACK, P], F32) for j in range(CT)] for g in range(HALVES)]
+        r = [kept("r%d" % g, [P, PACK, C], BF16) for g in range(HALVES)]
+        r_codes = [kept("r_codes%d" % g, [P, C], U32) for g in range(HALVES)]
+        r_scales = [kept("r_scales%d" % g, [P, C], U8) for g in range(HALVES)]
+        rt_codes = [kept("rt_codes%d" % g, [P, KP], U32) for g in range(HALVES)]
+        rt_scales = [kept("rt_scales%d" % g, [P, KP], U8) for g in range(HALVES)]
+        h_codes = [[kept("h_codes%d_%d" % (g, q), [P, N], U32) for q in range(FQ)] for g in range(HALVES)]
+        h_scales = [[kept("h_scales%d_%d" % (g, q), [P, N], U8) for q in range(FQ)] for g in range(HALVES)]
+
+        def load_scale_rows(engine, plane, scales, row0):
+            rows = scales.bitcast(I32).rearrange("g (q r) n -> r q g n", r=4)
+            for i in range(4):
+                engine.dma_start(out=plane[row0 + i : P : 32].bitcast(I32), in_=rows[i])
+
+        def load_hid(g):
+            src = hid_words.bitcast(I32).rearrange("k p n -> p k n")
+            nc.sync.dma_start(out=hid[g][:].bitcast(I32), in_=src[:, :, g * 256 : (g + 1) * 256])
+
+        def rows_of(x, g):
+            return x[g * KP : (g + 1) * KP, :].rearrange("(p t) n -> p t n", t=PACK)
+
+        def load_lam(g):
+            nc.sync.dma_start(out=lam_sb[g][:], in_=rows_of(lam, g))
+
+        def load_h(g, a):
+            nc.sync.dma_start(out=h_sb[g][a][:], in_=rows_of(h, g)[:, :, a * (F // 2) : (a + 1) * (F // 2)])
+
+        def load_d(g):
+            for a in range(2):
+                nc.sync.dma_start(out=d_sb[g][a][:], in_=rows_of(d, g)[:, 2 * a : 2 * a + 2, :])
+
+        nc.vector.memset(v_plane[:].rearrange("p g n -> p (g n)").bitcast(I32), 0)
+        nc.vector.memset(hid_plane[:].rearrange("p g n -> p (g n)").bitcast(I32), 0)
+        nc.vector.memset(w_plane[:].bitcast(I32), 0)
+        nc.vector.memset(vb_square[:], 0.0)
+
+        nc.sync.dma_start(out=vb_rows[:], in_=vb.rearrange("(j p) -> j p", p=P))
+        load_hid(0)
+        load_scale_rows(nc.sync, hid_plane, hid_scales, 0)
+        load_scale_rows(nc.gpsimd, v_plane, v_scales, 0)
+        nc.sync.dma_start(out=v[:].bitcast(I32), in_=v_words.bitcast(I32).rearrange("k p n -> p k n"))
+        make_identity(nc, ident[:])
+        load_lam(0)
+        load_h(0, 0)
+        load_scale_rows(nc.sync, w_plane[:].rearrange("p (g n) -> p g n", g=1), w_scales, W_ROW0)
+        load_h(0, 1)
+        load_hid(1)
+        nc.sync.dma_start(out=w[:].bitcast(I32), in_=w_words[0].rearrange("p n t -> p (n t)").bitcast(I32))
+        load_lam(1)
+        load_h(1, 0)
+        load_h(1, 1)
+        load_d(0)
+        load_d(1)
+
+        def bias_column():
+            nc.scalar.activation(out=vb_square[0:CT, :], in_=vb_rows[:], func=IDENT)
+            bank = scalar_bank()
+            nc.tensor.transpose(bank[:, 0:P], vb_square[:], ident[:])
+            nc.scalar.copy(out=vb_col[:], in_=bank[:, 0:CT])
+
+        def tangent(g, j):
+            bank = scalar_bank()
+            for k in range(FPASS):
+                nc.tensor.matmul_mx(
+                    out=bank[:],
+                    lhsT=v[:, k, 2 * P * j : 2 * P * (j + 1)].bitcast(FP4X4),
+                    lhsT_scale=v_plane[:, k, P * j : P * (j + 1)],
+                    rhs=hid[g][:, k, :].bitcast(FP4X4),
+                    rhs_scale=hid_plane[:, k, KP * g : KP * (g + 1)],
+                    start=(k == 0),
+                    stop=(k == FPASS - 1),
+                )
+            nc.scalar.activation(
+                out=zt[g][j][:], in_=bank[:].rearrange("p (m t) -> p t m", t=PACK), func=IDENT, bias=vb_col[:, j : j + 1]
+            )
+
+        def weigh(g):
+            for t in range(PACK):
+                bank = vector_bank()
+                for j in range(CT):
+                    nc.tensor.transpose(bank[:, P * j : P * (j + 1)], zt[g][j][:, t, :], ident[:])
+                nc.vector.tensor_tensor(out=r[g][:, t, :], in0=bank[:], in1=lam_sb[g][:, t, :], op=MULT)
+
+        def interleave(copy, src):
+            dst = staged()
+            copy(
+                out=dst[:].rearrange("p (c i) t -> p c t i", i=4),
+                in_=src.rearrange("p t (c i) -> p c t i", i=4),
+            )
+            return dst
+
+        def quantize(src, codes, scales):
+            nc.vector.quantize_mx(out=codes[:].bitcast(FP8X4), scales=scales[:], in_=src[:].rearrange("p c t -> p (c t)"))
+
+        def turn_r(g):
+            dst = staged()
+            dst_words = dst[:].rearrange("p c t -> p (c t)").bitcast(F32).rearrange("p (t s u) -> p t s u", t=PACK, u=2)
+            for a in range(2):
+                bank = scalar_bank()
+                view = bank[:].rearrange("p (t u s) -> p t u s", t=2, u=2)
+                for tt in range(2):
+                    words = r[g][:, 2 * a + tt, :].bitcast(F32)
+                    for u in range(2):
+                        nc.tensor.transpose(view[:, tt, u, :], words[:, u : 2 * P : 2], ident[:])
+                nc.scalar.copy(out=dst_words[:, 2 * a : 2 * a + 2], in_=view.rearrange("p t u s -> p t s u"))
+            return dst
+
+        def h_chunk(g, q):
+            return h_sb[g][q // 2][:, :, (q % 2) * N : (q % 2 + 1) * N]
+
+        def pull_back_hidden(g, t):
+            res = work.tile([P, F], F32, name="ga_out", tag="ga_out", bufs=4)
+            for q in range(FQ):
+                bank = vector_bank()
+                nc.tensor.matmul_mx(
+                    out=bank[:],
+                    lhsT=rt_codes[g][:, P * t : P * (t + 1)].bitcast(FP8X4),
+                    lhsT_scale=rt_scales[g][:, P * t : P * (t + 1)],
+                    rhs=w[:, PACK * N * q : PACK * N * (q + 1)].bitcast(FP8X4),
+                    rhs_scale=w_plane[W_ROW0:P, N * q : N * (q + 1)],
+                    start=True,
+                    stop=True,
+                )
+                nc.vector.tensor_tensor(
+                    out=res[:, N * q : N * (q + 1)], in0=bank[:], in1=d_sb[g][t // 2][:, t % 2, N * q : N * (q + 1)], op=MULT
+                )
+            nc.sync.dma_start(out=rows_of(out_1, g)[:, t, :], in_=res[:])
+
+        def pull_back_weights(q):
+            res = work.tile([P, PACK, C], F32, name="gw_out", tag="gw_out", bufs=2)
+            for i in range(N // P):
+                bank = scalar_bank()
+                for g in range(HALVES):
+                    nc.tensor.matmul_mx(
+                        out=bank[:],
+                        lhsT=h_codes[g][q][:, P * i : P * (i + 1)].bitcast(FP8X4),
+                        lhsT_scale=h_scales[g][q][:, P * i : P * (i + 1)],
+                        rhs=r_codes[g][:].bitcast(FP8X4),
+                        rhs_scale=r_scales[g][:],
+                        start=(g == 0),
+                        stop=(g == HALVES - 1),
+                    )
+                nc.scalar.copy(out=res[:, i, :], in_=bank[:])
+            nc.sync.dma_start(out=out_0[N * q : N * (q + 1), :].rearrange("(i m) c -> m i c", m=P), in_=res[:])
+
+        def quantize_h(g, q, src):
+            quantize(src, h_codes[g][q], h_scales[g][q])
+
+        vcopy = nc.vector.tensor_copy
+        scopy = nc.scalar.copy
+
+        bias_column()
+        for j in range(CT):
+            tangent(0, j)
+        s0 = interleave(vcopy, h_chunk(0, 0))
+        s1 = interleave(vcopy, h_chunk(0, 1))
+        quantize_h(0, 0, s0)
+        s2 = interleave(vcopy, h_chunk(0, 2))
+        quantize_h(0, 1, s1)
+        s3 = interleave(vcopy, h_chunk(0, 3))
+        quantize_h(0, 2, s2)
+        tangent(1, 0)
+        weigh(0)
+        tangent(1, 1)
+        tangent(1, 2)
+        rt0 = turn_r(0)
+        tangent(1, 3)
+        ri0 = interleave(vcopy, r[0][:])
+        quantize_h(0, 3, s3)
+        quantize(rt0, rt_codes[0], rt_scales[0])
+        quantize(ri0, r_codes[0], r_scales[0])
+        weigh(1)
+        s0 = interleave(scopy, h_chunk(1, 0))
+        pull_back_hidden(0, 0)
+        rt1 = turn_r(1)
+        ri1 = interleave(vcopy, r[1][:])
+        quantize_h(1, 0, s0)
+        quantize(rt1, rt_codes[1], rt_scales[1])
+        quantize(ri1, r_codes[1], r_scales[1])
+        s1 = interleave(scopy, h_chunk(1, 1))
+        s2 = interleave(scopy, h_chunk(1, 2))
+        pull_back_hidden(0, 1)
+        quantize_h(1, 1, s1)
+        pull_back_weights(0)
+        s3 = interleave(scopy, h_chunk(1, 3))
+        pull_back_hidden(0, 2)
+        quantize_h(1, 2, s2)
+        pull_back_weights(1)
+        pull_back_hidden(0, 3)
+        quantize_h(1, 3, s3)
+        pull_back_weights(2)
+        pull_back_hidden(1, 0)
+        pull_back_weights(3)
+        for t in range(1, PACK):
+            pull_back_hidden(1, t)

@@ -41,7 +41,7 @@ def tile_gauss_newton_product_s4_kernel(
             return keep.tile(shape, dtype, name=name, align_bytes=64)
 
         def staged():
-            return work.tile([P, N, PACK], BF16, name="staged", tag="staged", bufs=4, align_bytes=64)
+            return work.tile([P, N, PACK], BF16, name="staged", tag="staged", bufs=6, align_bytes=64)
 
         def scalar_bank():
             return psum.tile([P, N], F32, name="scalar_bank", tag="scalar_bank", bufs=4)
@@ -60,20 +60,20 @@ def tile_gauss_newton_product_s4_kernel(
         v = kept("v", [P, FPASS, 2 * C], U8)
         w = kept("w", [P, PACK * F], U8)
         lam_sb = [kept("lam%d" % g, [P, PACK, C], BF16) for g in range(HALVES)]
-        h_sb = [[kept("h%d_%d" % (g, a), [P, PACK, F // 2], BF16) for a in range(2)] for g in range(HALVES)]
+        h_sb = [kept("h%d" % g, [P, PACK, F], BF16) for g in range(HALVES)]
         d_sb = [[kept("d%d_%d" % (g, a), [P, 2, F], BF16) for a in range(2)] for g in range(HALVES)]
         zt = [[kept("zt%d_%d" % (g, j), [P, PACK, P], F32) for j in range(CT)] for g in range(HALVES)]
-        r = [kept("r%d" % g, [P, PACK, C], BF16) for g in range(HALVES)]
+        r = [kept("r%d" % g, [P, PACK * C], BF16) for g in range(HALVES)]
         r_codes = [kept("r_codes%d" % g, [P, C], U32) for g in range(HALVES)]
         r_scales = [kept("r_scales%d" % g, [P, C], U8) for g in range(HALVES)]
-        rt_codes = [kept("rt_codes%d" % g, [P, KP], U32) for g in range(HALVES)]
-        rt_scales = [kept("rt_scales%d" % g, [P, KP], U8) for g in range(HALVES)]
+        rt_codes = [[kept("rt_codes%d_%d" % (g, a), [P, 2 * P], U32) for a in range(2)] for g in range(HALVES)]
+        rt_scales = [[kept("rt_scales%d_%d" % (g, a), [P, 2 * P], U8) for a in range(2)] for g in range(HALVES)]
         h_codes = [[kept("h_codes%d_%d" % (g, q), [P, N], U32) for q in range(FQ)] for g in range(HALVES)]
         h_scales = [[kept("h_scales%d_%d" % (g, q), [P, N], U8) for q in range(FQ)] for g in range(HALVES)]
 
-        def load_scale_rows(engine, plane, scales, row0):
+        def load_scale_rows(engine, plane, scales, row0, which):
             rows = scales.bitcast(I32).rearrange("g (q r) n -> r q g n", r=4)
-            for i in range(4):
+            for i in which:
                 engine.dma_start(out=plane[row0 + i : P : 32].bitcast(I32), in_=rows[i])
 
         def load_hid(g):
@@ -86,35 +86,35 @@ def tile_gauss_newton_product_s4_kernel(
         def load_lam(g):
             nc.sync.dma_start(out=lam_sb[g][:], in_=rows_of(lam, g))
 
-        def load_h(g, a):
-            nc.sync.dma_start(out=h_sb[g][a][:], in_=rows_of(h, g)[:, :, a * (F // 2) : (a + 1) * (F // 2)])
+        def load_h(g):
+            nc.sync.dma_start(out=h_sb[g][:], in_=rows_of(h, g))
 
-        def load_d(g):
-            for a in range(2):
-                nc.sync.dma_start(out=d_sb[g][a][:], in_=rows_of(d, g)[:, 2 * a : 2 * a + 2, :])
+        def load_d(g, a):
+            nc.sync.dma_start(out=d_sb[g][a][:], in_=rows_of(d, g)[:, 2 * a : 2 * a + 2, :])
 
-        nc.vector.memset(v_plane[:].rearrange("p g n -> p (g n)").bitcast(I32), 0)
         nc.vector.memset(hid_plane[:].rearrange("p g n -> p (g n)").bitcast(I32), 0)
-        nc.vector.memset(w_plane[:].bitcast(I32), 0)
+        nc.vector.memset(v_plane[:].rearrange("p g n -> p (g n)").bitcast(I32), 0)
         nc.vector.memset(vb_square[:], 0.0)
 
-        nc.sync.dma_start(out=vb_rows[:], in_=vb.rearrange("(j p) -> j p", p=P))
+        nc.gpsimd.dma_start(out=vb_rows[:], in_=vb.rearrange("(j p) -> j p", p=P))
         load_hid(0)
-        load_scale_rows(nc.sync, hid_plane, hid_scales, 0)
-        load_scale_rows(nc.gpsimd, v_plane, v_scales, 0)
+        load_scale_rows(nc.sync, hid_plane, hid_scales, 0, range(4))
         nc.sync.dma_start(out=v[:].bitcast(I32), in_=v_words.bitcast(I32).rearrange("k p n -> p k n"))
+        load_scale_rows(nc.sync, v_plane, v_scales, 0, range(2))
+        load_scale_rows(nc.gpsimd, v_plane, v_scales, 0, range(2, 4))
         make_identity(nc, ident[:])
+        nc.gpsimd.memset(w_plane[:].bitcast(I32), 0)
+        load_scale_rows(nc.gpsimd, w_plane[:].rearrange("p (g n) -> p g n", g=1), w_scales, W_ROW0, range(4))
+        load_h(0)
         load_lam(0)
-        load_h(0, 0)
-        load_scale_rows(nc.sync, w_plane[:].rearrange("p (g n) -> p g n", g=1), w_scales, W_ROW0)
-        load_h(0, 1)
         load_hid(1)
         nc.sync.dma_start(out=w[:].bitcast(I32), in_=w_words[0].rearrange("p n t -> p (n t)").bitcast(I32))
+        load_d(0, 0)
         load_lam(1)
-        load_h(1, 0)
-        load_h(1, 1)
-        load_d(0)
-        load_d(1)
+        load_h(1)
+        load_d(0, 1)
+        load_d(1, 0)
+        load_d(1, 1)
 
         def bias_column():
             nc.scalar.activation(out=vb_square[0:CT, :], in_=vb_rows[:], func=IDENT)
@@ -143,7 +143,7 @@ def tile_gauss_newton_product_s4_kernel(
                 bank = vector_bank()
                 for j in range(CT):
                     nc.tensor.transpose(bank[:, P * j : P * (j + 1)], zt[g][j][:, t, :], ident[:])
-                nc.vector.tensor_tensor(out=r[g][:, t, :], in0=bank[:], in1=lam_sb[g][:, t, :], op=MULT)
+                nc.vector.tensor_tensor(out=r[g][:, C * t : C * (t + 1)], in0=bank[:], in1=lam_sb[g][:, t, :], op=MULT)
 
         def interleave(copy, src):
             dst = staged()
@@ -156,30 +156,41 @@ def tile_gauss_newton_product_s4_kernel(
         def quantize(src, codes, scales):
             nc.vector.quantize_mx(out=codes[:].bitcast(FP8X4), scales=scales[:], in_=src[:].rearrange("p c t -> p (c t)"))
 
-        def turn_r(g):
-            dst = staged()
-            dst_words = dst[:].rearrange("p c t -> p (c t)").bitcast(F32).rearrange("p (t s u) -> p t s u", t=PACK, u=2)
-            for a in range(2):
-                bank = scalar_bank()
-                view = bank[:].rearrange("p (t u s) -> p t u s", t=2, u=2)
-                for tt in range(2):
-                    words = r[g][:, 2 * a + tt, :].bitcast(F32)
-                    for u in range(2):
-                        nc.tensor.transpose(view[:, tt, u, :], words[:, u : 2 * P : 2], ident[:])
-                nc.scalar.copy(out=dst_words[:, 2 * a : 2 * a + 2], in_=view.rearrange("p t u s -> p t s u"))
+        def turn_r(g, a):
+            dst = work.tile([P, 2 * P, PACK], BF16, name="turned", tag="turned", bufs=2, align_bytes=64)
+            dst_words = dst[:].rearrange("p c t -> p (c t)").bitcast(F32).rearrange("p (t s u) -> p t s u", t=2, u=2)
+            bank = scalar_bank()
+            view = bank[:].rearrange("p (t u s) -> p t u s", t=2, u=2)
+            for tt in range(2):
+                t = 2 * a + tt
+                words = r[g][:, C * t : C * (t + 1)].bitcast(F32)
+                for u in range(2):
+                    nc.tensor.transpose(view[:, tt, u, :], words[:, u : 2 * P : 2], ident[:])
+            nc.scalar.copy(out=dst_words, in_=view.rearrange("p t u s -> p t s u"))
             return dst
 
-        def h_chunk(g, q):
-            return h_sb[g][q // 2][:, :, (q % 2) * N : (q % 2 + 1) * N]
+        def quantize_rt(g, a, src):
+            quantize(src, rt_codes[g][a], rt_scales[g][a])
+
+        def r_rows(g):
+            return r[g][:].rearrange("p (t c) -> p t c", t=PACK)
+
+        def interleave_h(copy, g, q):
+            dst = staged()
+            copy(
+                out=dst[:].rearrange("p (i m) t -> p m t i", i=PACK),
+                in_=h_sb[g][:, :, N * q : N * (q + 1)].rearrange("p t (m i) -> p m t i", i=PACK),
+            )
+            return dst
 
         def pull_back_hidden(g, t):
-            res = work.tile([P, F], F32, name="ga_out", tag="ga_out", bufs=4)
+            res = work.tile([P, F], F32, name="ga_out", tag="out", bufs=6)
             for q in range(FQ):
                 bank = vector_bank()
                 nc.tensor.matmul_mx(
                     out=bank[:],
-                    lhsT=rt_codes[g][:, P * t : P * (t + 1)].bitcast(FP8X4),
-                    lhsT_scale=rt_scales[g][:, P * t : P * (t + 1)],
+                    lhsT=rt_codes[g][t // 2][:, P * (t % 2) : P * (t % 2 + 1)].bitcast(FP8X4),
+                    lhsT_scale=rt_scales[g][t // 2][:, P * (t % 2) : P * (t % 2 + 1)],
                     rhs=w[:, PACK * N * q : PACK * N * (q + 1)].bitcast(FP8X4),
                     rhs_scale=w_plane[W_ROW0:P, N * q : N * (q + 1)],
                     start=True,
@@ -190,10 +201,10 @@ def tile_gauss_newton_product_s4_kernel(
                 )
             nc.sync.dma_start(out=rows_of(out_1, g)[:, t, :], in_=res[:])
 
-        def pull_back_weights(q):
-            res = work.tile([P, PACK, C], F32, name="gw_out", tag="gw_out", bufs=2)
+        def pull_back_weights(q, new_bank, copy):
+            res = work.tile([P, PACK, C], F32, name="gw_out", tag="out", bufs=6)
             for i in range(N // P):
-                bank = scalar_bank()
+                bank = new_bank()
                 for g in range(HALVES):
                     nc.tensor.matmul_mx(
                         out=bank[:],
@@ -204,8 +215,8 @@ def tile_gauss_newton_product_s4_kernel(
                         start=(g == 0),
                         stop=(g == HALVES - 1),
                     )
-                nc.scalar.copy(out=res[:, i, :], in_=bank[:])
-            nc.sync.dma_start(out=out_0[N * q : N * (q + 1), :].rearrange("(i m) c -> m i c", m=P), in_=res[:])
+                copy(out=res[:, i, :], in_=bank[:])
+            nc.sync.dma_start(out=out_0[N * q : N * (q + 1), :].rearrange("(m i) c -> m i c", m=P), in_=res[:])
 
         def quantize_h(g, q, src):
             quantize(src, h_codes[g][q], h_scales[g][q])
@@ -216,44 +227,49 @@ def tile_gauss_newton_product_s4_kernel(
         bias_column()
         for j in range(CT):
             tangent(0, j)
-        s0 = interleave(vcopy, h_chunk(0, 0))
-        s1 = interleave(vcopy, h_chunk(0, 1))
-        quantize_h(0, 0, s0)
-        s2 = interleave(vcopy, h_chunk(0, 2))
-        quantize_h(0, 1, s1)
-        s3 = interleave(vcopy, h_chunk(0, 3))
-        quantize_h(0, 2, s2)
-        tangent(1, 0)
+        s00 = interleave_h(vcopy, 0, 0)
+        s01 = interleave_h(vcopy, 0, 1)
+        s02 = interleave_h(scopy, 0, 2)
         weigh(0)
+        tangent(1, 0)
+        rta = turn_r(0, 0)
+        rtb = turn_r(0, 1)
         tangent(1, 1)
-        tangent(1, 2)
-        rt0 = turn_r(0)
-        tangent(1, 3)
-        ri0 = interleave(vcopy, r[0][:])
-        quantize_h(0, 3, s3)
-        quantize(rt0, rt_codes[0], rt_scales[0])
-        quantize(ri0, r_codes[0], r_scales[0])
-        weigh(1)
-        s0 = interleave(scopy, h_chunk(1, 0))
+        s03 = interleave_h(vcopy, 0, 3)
+        quantize_rt(0, 0, rta)
+        quantize_rt(0, 1, rtb)
+        quantize_h(0, 0, s00)
+        ri0 = interleave(scopy, r_rows(0))
         pull_back_hidden(0, 0)
-        rt1 = turn_r(1)
-        ri1 = interleave(vcopy, r[1][:])
-        quantize_h(1, 0, s0)
-        quantize(rt1, rt_codes[1], rt_scales[1])
-        quantize(ri1, r_codes[1], r_scales[1])
-        s1 = interleave(scopy, h_chunk(1, 1))
-        s2 = interleave(scopy, h_chunk(1, 2))
+        tangent(1, 2)
+        tangent(1, 3)
+        quantize_h(0, 1, s01)
+        quantize(ri0, r_codes[0], r_scales[0])
         pull_back_hidden(0, 1)
-        quantize_h(1, 1, s1)
-        pull_back_weights(0)
-        s3 = interleave(scopy, h_chunk(1, 3))
+        weigh(1)
+        s10 = interleave_h(scopy, 1, 0)
         pull_back_hidden(0, 2)
-        quantize_h(1, 2, s2)
-        pull_back_weights(1)
+        ri1 = interleave(scopy, r_rows(1))
+        rta = turn_r(1, 0)
+        rtb = turn_r(1, 1)
+        quantize_h(1, 0, s10)
+        quantize(ri1, r_codes[1], r_scales[1])
         pull_back_hidden(0, 3)
-        quantize_h(1, 3, s3)
-        pull_back_weights(2)
+        pull_back_weights(0, scalar_bank, scopy)
+        quantize_rt(1, 0, rta)
+        quantize_rt(1, 1, rtb)
+        s11 = interleave_h(scopy, 1, 1)
         pull_back_hidden(1, 0)
-        pull_back_weights(3)
-        for t in range(1, PACK):
-            pull_back_hidden(1, t)
+        quantize_h(0, 2, s02)
+        quantize_h(1, 1, s11)
+        s12 = interleave_h(scopy, 1, 2)
+        pull_back_hidden(1, 1)
+        pull_back_weights(1, scalar_bank, scopy)
+        quantize_h(0, 3, s03)
+        quantize_h(1, 2, s12)
+        s13 = interleave_h(scopy, 1, 3)
+        pull_back_hidden(1, 2)
+        pull_back_weights(2, scalar_bank, scopy)
+        quantize_h(1, 3, s13)
+        pull_back_hidden(1, 3)
+        pull_back_weights(3, scalar_bank, scopy)

@@ -56,11 +56,12 @@ def tile_gauss_newton_product_s4_kernel(
         hid_plane = kept("hid_plane", [P, FPASS, B], U8)
         v_plane = kept("v_plane", [P, FPASS, C], U8)
         w_plane = kept("w_plane", [P, F], U8)
-        hid = [kept("hid%d" % g, [P, FPASS, 2 * KP], U8) for g in range(HALVES)]
+        hid = [kept("hid%d" % a, [P, 2, 2 * B], U8) for a in range(FPASS // 2)]
         v = kept("v", [P, FPASS, 2 * C], U8)
         w = kept("w", [P, PACK * F], U8)
         lam_sb = [kept("lam%d" % g, [P, PACK, C], BF16) for g in range(HALVES)]
-        h_sb = [kept("h%d" % g, [P, PACK, F], BF16) for g in range(HALVES)]
+        h_width = (F // 2, F)
+        h_sb = [[kept("h%d_%d" % (g, a), [P, PACK, h_width[g]], BF16) for a in range(F // h_width[g])] for g in range(HALVES)]
         d_sb = [[kept("d%d_%d" % (g, a), [P, 2, F], BF16) for a in range(2)] for g in range(HALVES)]
         zt = [[kept("zt%d_%d" % (g, j), [P, PACK, P], F32) for j in range(CT)] for g in range(HALVES)]
         r = [kept("r%d" % g, [P, PACK * C], BF16) for g in range(HALVES)]
@@ -78,7 +79,7 @@ def tile_gauss_newton_product_s4_kernel(
 
         def load_hid(g):
             src = hid_words.bitcast(I32).rearrange("k p n -> p k n")
-            nc.sync.dma_start(out=hid[g][:].bitcast(I32), in_=src[:, :, g * 256 : (g + 1) * 256])
+            nc.sync.dma_start(out=hid[g][:].bitcast(I32), in_=src[:, 2 * g : 2 * g + 2, :])
 
         def rows_of(x, g):
             return x[g * KP : (g + 1) * KP, :].rearrange("(p t) n -> p t n", t=PACK)
@@ -87,7 +88,8 @@ def tile_gauss_newton_product_s4_kernel(
             nc.sync.dma_start(out=lam_sb[g][:], in_=rows_of(lam, g))
 
         def load_h(g):
-            nc.sync.dma_start(out=h_sb[g][:], in_=rows_of(h, g))
+            for a in range(F // h_width[g]):
+                nc.sync.dma_start(out=h_sb[g][a][:], in_=rows_of(h, g)[:, :, h_width[g] * a : h_width[g] * (a + 1)])
 
         def load_d(g, a):
             nc.sync.dma_start(out=d_sb[g][a][:], in_=rows_of(d, g)[:, 2 * a : 2 * a + 2, :])
@@ -105,9 +107,9 @@ def tile_gauss_newton_product_s4_kernel(
         make_identity(nc, ident[:])
         nc.gpsimd.memset(w_plane[:].bitcast(I32), 0)
         load_scale_rows(nc.gpsimd, w_plane[:].rearrange("p (g n) -> p g n", g=1), w_scales, W_ROW0, range(4))
+        load_hid(1)
         load_h(0)
         load_lam(0)
-        load_hid(1)
         nc.sync.dma_start(out=w[:].bitcast(I32), in_=w_words[0].rearrange("p n t -> p (n t)").bitcast(I32))
         load_d(0, 0)
         load_lam(1)
@@ -129,7 +131,7 @@ def tile_gauss_newton_product_s4_kernel(
                     out=bank[:],
                     lhsT=v[:, k, 2 * P * j : 2 * P * (j + 1)].bitcast(FP4X4),
                     lhsT_scale=v_plane[:, k, P * j : P * (j + 1)],
-                    rhs=hid[g][:, k, :].bitcast(FP4X4),
+                    rhs=hid[k // 2][:, k % 2, 2 * KP * g : 2 * KP * (g + 1)].bitcast(FP4X4),
                     rhs_scale=hid_plane[:, k, KP * g : KP * (g + 1)],
                     start=(k == 0),
                     stop=(k == FPASS - 1),
@@ -177,9 +179,10 @@ def tile_gauss_newton_product_s4_kernel(
 
         def interleave_h(copy, g, q):
             dst = staged()
+            a, col = divmod(N * q, h_width[g])
             copy(
                 out=dst[:].rearrange("p (i m) t -> p m t i", i=PACK),
-                in_=h_sb[g][:, :, N * q : N * (q + 1)].rearrange("p t (m i) -> p m t i", i=PACK),
+                in_=h_sb[g][a][:, :, col : col + N].rearrange("p t (m i) -> p m t i", i=PACK),
             )
             return dst
 
@@ -229,47 +232,47 @@ def tile_gauss_newton_product_s4_kernel(
             tangent(0, j)
         s00 = interleave_h(vcopy, 0, 0)
         s01 = interleave_h(vcopy, 0, 1)
-        s02 = interleave_h(scopy, 0, 2)
+        s02 = interleave_h(vcopy, 0, 2)
+        s03 = interleave_h(scopy, 0, 3)
         weigh(0)
         tangent(1, 0)
+        tangent(1, 1)
         rta = turn_r(0, 0)
         rtb = turn_r(0, 1)
-        tangent(1, 1)
-        s03 = interleave_h(vcopy, 0, 3)
+        tangent(1, 2)
+        quantize_h(0, 0, s00)
+        ri0 = interleave(vcopy, r_rows(0))
+        quantize_h(0, 1, s01)
         quantize_rt(0, 0, rta)
         quantize_rt(0, 1, rtb)
-        quantize_h(0, 0, s00)
-        ri0 = interleave(scopy, r_rows(0))
-        pull_back_hidden(0, 0)
-        tangent(1, 2)
-        tangent(1, 3)
-        quantize_h(0, 1, s01)
         quantize(ri0, r_codes[0], r_scales[0])
-        pull_back_hidden(0, 1)
+        pull_back_hidden(0, 0)
+        tangent(1, 3)
+        quantize_h(0, 2, s02)
         weigh(1)
         s10 = interleave_h(scopy, 1, 0)
-        pull_back_hidden(0, 2)
+        pull_back_hidden(0, 1)
         ri1 = interleave(scopy, r_rows(1))
         rta = turn_r(1, 0)
         rtb = turn_r(1, 1)
         quantize_h(1, 0, s10)
         quantize(ri1, r_codes[1], r_scales[1])
-        pull_back_hidden(0, 3)
+        pull_back_hidden(0, 2)
         pull_back_weights(0, scalar_bank, scopy)
         quantize_rt(1, 0, rta)
         quantize_rt(1, 1, rtb)
         s11 = interleave_h(scopy, 1, 1)
-        pull_back_hidden(1, 0)
-        quantize_h(0, 2, s02)
+        pull_back_hidden(0, 3)
         quantize_h(1, 1, s11)
         s12 = interleave_h(scopy, 1, 2)
-        pull_back_hidden(1, 1)
+        pull_back_hidden(1, 0)
         pull_back_weights(1, scalar_bank, scopy)
-        quantize_h(0, 3, s03)
         quantize_h(1, 2, s12)
+        quantize_h(0, 3, s03)
+        pull_back_hidden(1, 1)
+        pull_back_weights(2, scalar_bank, scopy)
         s13 = interleave_h(scopy, 1, 3)
         pull_back_hidden(1, 2)
-        pull_back_weights(2, scalar_bank, scopy)
         quantize_h(1, 3, s13)
         pull_back_hidden(1, 3)
         pull_back_weights(3, scalar_bank, scopy)

@@ -94,22 +94,21 @@ def tile_gauss_newton_product_s4_kernel(
         def load_d(g, a):
             nc.sync.dma_start(out=d_sb[g][a][:], in_=rows_of(d, g)[:, 2 * a : 2 * a + 2, :])
 
-        nc.vector.memset(hid_plane[:].rearrange("p g n -> p (g n)").bitcast(I32), 0)
         nc.vector.memset(v_plane[:].rearrange("p g n -> p (g n)").bitcast(I32), 0)
+        nc.vector.memset(hid_plane[:].rearrange("p g n -> p (g n)").bitcast(I32), 0)
         nc.vector.memset(vb_square[:], 0.0)
+        nc.vector.memset(w_plane[:].bitcast(I32), 0)
 
-        nc.gpsimd.dma_start(out=vb_rows[:], in_=vb.rearrange("(j p) -> j p", p=P))
-        load_hid(0)
-        load_scale_rows(nc.sync, hid_plane, hid_scales, 0, range(4))
-        nc.sync.dma_start(out=v[:].bitcast(I32), in_=v_words.bitcast(I32).rearrange("k p n -> p k n"))
-        load_scale_rows(nc.sync, v_plane, v_scales, 0, range(2))
-        load_scale_rows(nc.gpsimd, v_plane, v_scales, 0, range(2, 4))
         make_identity(nc, ident[:])
-        nc.gpsimd.memset(w_plane[:].bitcast(I32), 0)
-        load_scale_rows(nc.gpsimd, w_plane[:].rearrange("p (g n) -> p g n", g=1), w_scales, W_ROW0, range(4))
+        nc.sync.dma_start(out=vb_rows[:], in_=vb.rearrange("(j p) -> j p", p=P))
+        load_hid(0)
+        load_scale_rows(nc.sync, v_plane, v_scales, 0, range(4))
+        nc.sync.dma_start(out=v[:].bitcast(I32), in_=v_words.bitcast(I32).rearrange("k p n -> p k n"))
+        load_scale_rows(nc.sync, hid_plane, hid_scales, 0, range(4))
         load_hid(1)
         load_h(0)
         load_lam(0)
+        load_scale_rows(nc.sync, w_plane[:].rearrange("p (g n) -> p g n", g=1), w_scales, W_ROW0, range(4))
         nc.sync.dma_start(out=w[:].bitcast(I32), in_=w_words[0].rearrange("p n t -> p (n t)").bitcast(I32))
         load_d(0, 0)
         load_lam(1)

from contextlib import ExitStack

import concourse.mybir as mybir
from concourse.masks import make_identity

B, F, C = 1024, 2048, 512
FLOPS = 3 * 2 * B * F * C

F32 = mybir.dt.float32
BF16 = mybir.dt.bfloat16
I32 = mybir.dt.int32
U32 = mybir.dt.uint32
U8 = mybir.dt.uint8
FP8X4 = mybir.dt.float8_e4m3fn_x4
FP4X4 = mybir.dt.float4_e2m1fn_x4
MULT = mybir.AluOpType.mult
IDENT = mybir.ActivationFunctionType.Identity

P = 128
PACK = 4
KP = P * PACK
N = 512
HALVES = B // KP
FPASS = F // KP
CT = C // P
FQ = F // N
W_ROW0 = 4


def tile_gauss_newton_product_s4_kernel(
    tc, hid_words, hid_scales, v_words, v_scales, vb, lam, h, w_words, w_scales, d, out_0, out_1
):
    nc = tc.nc
    with ExitStack() as ctx:
        keep = ctx.enter_context(tc.tile_pool(name="keep", bufs=1))
        work = ctx.enter_context(tc.tile_pool(name="work", bufs=1))
        psum = ctx.enter_context(tc.psum_pool(name="psum", bufs=1))
        ctx.enter_context(tc.manual_schedule())

        def kept(name, shape, dtype):
            return keep.tile(shape, dtype, name=name, align_bytes=64)

        def staged():
            return work.tile([P, N, PACK], BF16, name="staged", tag="staged", bufs=6, align_bytes=64)

        def scalar_bank():
            return psum.tile([P, N], F32, name="scalar_bank", tag="scalar_bank", bufs=4)

        def vector_bank():
            return psum.tile([P, N], F32, name="vector_bank", tag="vector_bank", bufs=4)

        ident = kept("ident", [P, P], F32)
        vb_rows = kept("vb_rows", [CT, P], BF16)
        vb_square = kept("vb_square", [P, P], F32)
        vb_col = kept("vb_col", [P, CT], F32)
        hid_plane = kept("hid_plane", [P, FPASS, B], U8)
        v_plane = kept("v_plane", [P, FPASS, C], U8)
        w_plane = kept("w_plane", [P, F], U8)
        hid = [kept("hid%d" % a, [P, 2, 2 * B], U8) for a in range(FPASS // 2)]
        v = kept("v", [P, FPASS, 2 * C], U8)
        w = kept("w", [P, PACK * F], U8)
        lam_sb = [kept("lam%d" % g, [P, PACK, C], BF16) for g in range(HALVES)]
        h_width = (F // 2, F)
        h_sb = [[kept("h%d_%d" % (g, a), [P, PACK, h_width[g]], BF16) for a in range(F // h_width[g])] for g in range(HALVES)]
        d_sb = [[kept("d%d_%d" % (g, a), [P, 2, F], BF16) for a in range(2)] for g in range(HALVES)]
        zt = [[kept("zt%d_%d" % (g, j), [P, PACK, P], F32) for j in range(CT)] for g in range(HALVES)]
        r = [kept("r%d" % g, [P, PACK * C], BF16) for g in range(HALVES)]
        r_codes = [kept("r_codes%d" % g, [P, C], U32) for g in range(HALVES)]
        r_scales = [kept("r_scales%d" % g, [P, C], U8) for g in range(HALVES)]
        rt_codes = [[kept("rt_codes%d_%d" % (g, a), [P, 2 * P], U32) for a in range(2)] for g in range(HALVES)]
        rt_scales = [[kept("rt_scales%d_%d" % (g, a), [P, 2 * P], U8) for a in range(2)] for g in range(HALVES)]
        h_codes = [[kept("h_codes%d_%d" % (g, q), [P, N], U32) for q in range(FQ)] for g in range(HALVES)]
        h_scales = [[kept("h_scales%d_%d" % (g, q), [P, N], U8) for q in range(FQ)] for g in range(HALVES)]

        def load_scale_rows(engine, plane, scales, row0, which):
            rows = scales.bitcast(I32).rearrange("g (q r) n -> r q g n", r=4)
            for i in which:
                engine.dma_start(out=plane[row0 + i : P : 32].bitcast(I32), in_=rows[i])

        def load_hid(g):
            src = hid_words.bitcast(I32).rearrange("k p n -> p k n")
            nc.sync.dma_start(out=hid[g][:].bitcast(I32), in_=src[:, 2 * g : 2 * g + 2, :])

        def rows_of(x, g):
            return x[g * KP : (g + 1) * KP, :].rearrange("(p t) n -> p t n", t=PACK)

        def load_lam(g):
            nc.sync.dma_start(out=lam_sb[g][:], in_=rows_of(lam, g))

        def load_h(g):
            for a in range(F // h_width[g]):
                nc.sync.dma_start(out=h_sb[g][a][:], in_=rows_of(h, g)[:, :, h_width[g] * a : h_width[g] * (a + 1)])

        def load_d(g, a):
            nc.sync.dma_start(out=d_sb[g][a][:], in_=rows_of(d, g)[:, 2 * a : 2 * a + 2, :])

        nc.vector.memset(v_plane[:].rearrange("p g n -> p (g n)").bitcast(I32), 0)
        nc.vector.memset(hid_plane[:].rearrange("p g n -> p (g n)").bitcast(I32), 0)
        nc.vector.memset(vb_square[:], 0.0)
        nc.vector.memset(w_plane[:].bitcast(I32), 0)

        make_identity(nc, ident[:])
        nc.sync.dma_start(out=vb_rows[:], in_=vb.rearrange("(j p) -> j p", p=P))
        load_hid(0)
        load_scale_rows(nc.sync, v_plane, v_scales, 0, range(4))
        nc.sync.dma_start(out=v[:].bitcast(I32), in_=v_words.bitcast(I32).rearrange("k p n -> p k n"))
        load_scale_rows(nc.sync, hid_plane, hid_scales, 0, range(4))
        load_hid(1)
        load_h(0)
        load_lam(0)
        load_scale_rows(nc.sync, w_plane[:].rearrange("p (g n) -> p g n", g=1), w_scales, W_ROW0, range(4))
        nc.sync.dma_start(out=w[:].bitcast(I32), in_=w_words[0].rearrange("p n t -> p (n t)").bitcast(I32))
        load_d(0, 0)
        load_lam(1)
        load_h(1)
        load_d(0, 1)
        load_d(1, 0)
        load_d(1, 1)

        def bias_column():
            nc.scalar.activation(out=vb_square[0:CT, :], in_=vb_rows[:], func=IDENT)
            bank = scalar_bank()
            nc.tensor.transpose(bank[:, 0:P], vb_square[:], ident[:])
            nc.scalar.copy(out=vb_col[:], in_=bank[:, 0:CT])

        def tangent(g, j):
            bank = scalar_bank()
            for k in range(FPASS):
                nc.tensor.matmul_mx(
                    out=bank[:],
                    lhsT=v[:, k, 2 * P * j : 2 * P * (j + 1)].bitcast(FP4X4),
                    lhsT_scale=v_plane[:, k, P * j : P * (j + 1)],
                    rhs=hid[k // 2][:, k % 2, 2 * KP * g : 2 * KP * (g + 1)].bitcast(FP4X4),
                    rhs_scale=hid_plane[:, k, KP * g : KP * (g + 1)],
                    start=(k == 0),
                    stop=(k == FPASS - 1),
                )
            nc.scalar.activation(
                out=zt[g][j][:], in_=bank[:].rearrange("p (m t) -> p t m", t=PACK), func=IDENT, bias=vb_col[:, j : j + 1]
            )

        def weigh(g):
            for t in range(PACK):
                bank = vector_bank()
                for j in range(CT):
                    nc.tensor.transpose(bank[:, P * j : P * (j + 1)], zt[g][j][:, t, :], ident[:])
                nc.vector.tensor_tensor(out=r[g][:, C * t : C * (t + 1)], in0=bank[:], in1=lam_sb[g][:, t, :], op=MULT)

        def interleave(copy, src):
            dst = staged()
            copy(
                out=dst[:].rearrange("p (c i) t -> p c t i", i=4),
                in_=src.rearrange("p t (c i) -> p c t i", i=4),
            )
            return dst

        def quantize(src, codes, scales):
            nc.vector.quantize_mx(out=codes[:].bitcast(FP8X4), scales=scales[:], in_=src[:].rearrange("p c t -> p (c t)"))

        def turn_r(g, a):
            dst = work.tile([P, 2 * P, PACK], BF16, name="turned", tag="turned", bufs=2, align_bytes=64)
            dst_words = dst[:].rearrange("p c t -> p (c t)").bitcast(F32).rearrange("p (t s u) -> p t s u", t=2, u=2)
            bank = scalar_bank()
            view = bank[:].rearrange("p (t u s) -> p t u s", t=2, u=2)
            for tt in range(2):
                t = 2 * a + tt
                words = r[g][:, C * t : C * (t + 1)].bitcast(F32)
                for u in range(2):
                    nc.tensor.transpose(view[:, tt, u, :], words[:, u : 2 * P : 2], ident[:])
            nc.scalar.copy(out=dst_words, in_=view.rearrange("p t u s -> p t s u"))
            return dst

        def quantize_rt(g, a, src):
            quantize(src, rt_codes[g][a], rt_scales[g][a])

        def r_rows(g):
            return r[g][:].rearrange("p (t c) -> p t c", t=PACK)

        def interleave_h(copy, g, q):
            dst = staged()
            a, col = divmod(N * q, h_width[g])
            copy(
                out=dst[:].rearrange("p (i m) t -> p m t i", i=PACK),
                in_=h_sb[g][a][:, :, col : col + N].rearrange("p t (m i) -> p m t i", i=PACK),
            )
            return dst

        def pull_back_hidden(g, t):
            res = work.tile([P, F], F32, name="ga_out", tag="out", bufs=6)
            for q in range(FQ):
                bank = vector_bank()
                nc.tensor.matmul_mx(
                    out=bank[:],
                    lhsT=rt_codes[g][t // 2][:, P * (t % 2) : P * (t % 2 + 1)].bitcast(FP8X4),
                    lhsT_scale=rt_scales[g][t // 2][:, P * (t % 2) : P * (t % 2 + 1)],
                    rhs=w[:, PACK * N * q : PACK * N * (q + 1)].bitcast(FP8X4),
                    rhs_scale=w_plane[W_ROW0:P, N * q : N * (q + 1)],
                    start=True,
                    stop=True,
                )
                nc.vector.tensor_tensor(
                    out=res[:, N * q : N * (q + 1)], in0=bank[:], in1=d_sb[g][t // 2][:, t % 2, N * q : N * (q + 1)], op=MULT
                )
            nc.sync.dma_start(out=rows_of(out_1, g)[:, t, :], in_=res[:])

        def pull_back_weights(q, new_bank, copy):
            res = work.tile([P, PACK, C], F32, name="gw_out", tag="out", bufs=6)
            for i in range(N // P):
                bank = new_bank()
                for g in range(HALVES):
                    nc.tensor.matmul_mx(
                        out=bank[:],
                        lhsT=h_codes[g][q][:, P * i : P * (i + 1)].bitcast(FP8X4),
                        lhsT_scale=h_scales[g][q][:, P * i : P * (i + 1)],
                        rhs=r_codes[g][:].bitcast(FP8X4),
                        rhs_scale=r_scales[g][:],
                        start=(g == 0),
                        stop=(g == HALVES - 1),
                    )
                copy(out=res[:, i, :], in_=bank[:])
            nc.sync.dma_start(out=out_0[N * q : N * (q + 1), :].rearrange("(m i) c -> m i c", m=P), in_=res[:])

        def quantize_h(g, q, src):
            quantize(src, h_codes[g][q], h_scales[g][q])

        vcopy = nc.vector.tensor_copy
        scopy = nc.scalar.copy

        bias_column()
        for j in range(CT):
            tangent(0, j)
        s00 = interleave_h(vcopy, 0, 0)
        s01 = interleave_h(vcopy, 0, 1)
        s02 = interleave_h(vcopy, 0, 2)
        s03 = interleave_h(scopy, 0, 3)
        weigh(0)
        tangent(1, 0)
        tangent(1, 1)
        rta = turn_r(0, 0)
        rtb = turn_r(0, 1)
        tangent(1, 2)
        quantize_h(0, 0, s00)
        ri0 = interleave(vcopy, r_rows(0))
        quantize_h(0, 1, s01)
        quantize_rt(0, 0, rta)
        quantize_rt(0, 1, rtb)
        quantize(ri0, r_codes[0], r_scales[0])
        pull_back_hidden(0, 0)
        tangent(1, 3)
        quantize_h(0, 2, s02)
        weigh(1)
        s10 = interleave_h(scopy, 1, 0)
        pull_back_hidden(0, 1)
        ri1 = interleave(scopy, r_rows(1))
        rta = turn_r(1, 0)
        rtb = turn_r(1, 1)
        quantize_h(1, 0, s10)
        quantize(ri1, r_codes[1], r_scales[1])
        pull_back_hidden(0, 2)
        pull_back_weights(0, scalar_bank, scopy)
        quantize_rt(1, 0, rta)
        quantize_rt(1, 1, rtb)
        s11 = interleave_h(scopy, 1, 1)
        pull_back_hidden(0, 3)
        quantize_h(1, 1, s11)
        s12 = interleave_h(scopy, 1, 2)
        pull_back_hidden(1, 0)
        pull_back_weights(1, scalar_bank, scopy)
        quantize_h(1, 2, s12)
        quantize_h(0, 3, s03)
        pull_back_hidden(1, 1)
        pull_back_weights(2, scalar_bank, scopy)
        s13 = interleave_h(scopy, 1, 3)
        pull_back_hidden(1, 2)
        quantize_h(1, 3, s13)
        pull_back_hidden(1, 3)
        pull_back_weights(3, scalar_bank, scopy)
